import numpy as np
import ml_dtypes


def mxq(x, axis, fmt="e4m3"):
    dtype, down = {"e4m3": (ml_dtypes.float8_e4m3fn, 7), "e5m2": (ml_dtypes.float8_e5m2, 14)}[fmt]
    v = np.moveaxis(np.asarray(x, np.float32).astype(ml_dtypes.bfloat16).astype(np.float64), axis, -1)
    blocks = v.reshape(v.shape[:-1] + (-1, 32))
    amax = np.abs(blocks).max(-1, keepdims=True)
    byte = np.maximum(np.where(amax > 0, np.frexp(amax)[1] - 1 + 127, 0) - down, 1)
    scale = np.exp2(byte - 127.0)
    codes = (blocks / scale).astype(np.float32).astype(dtype).astype(np.float64)
    return np.moveaxis((codes * scale).reshape(v.shape), -1, axis)


WIDE = False


def mx_kscale(k):
    if not WIDE:
        return np.ones(k)
    levels = np.array([10, -10, 5, -5, 0])
    if k % 512:
        return np.exp2(np.random.permutation(np.resize(levels, k // 32))).repeat(32)
    a = np.empty((k // 512, 16))
    for p in range(k // 512):
        a[p, :8] = np.random.permutation(np.resize(levels, 8))
        for g in range(8):
            far = levels[np.abs(levels - a[p, g]) >= 10]
            a[p, g + 8] = far[np.random.randint(len(far))]
    return np.exp2(a.ravel()).repeat(32)


def f64(x):
    return np.asarray(x).astype(np.float64)


def striped8(idx):
    return np.asarray(idx).reshape(8, -1, 16).transpose(0, 2, 1).reshape(128, -1).astype(np.uint16)


def unstriped8(offs):
    return offs.reshape(8, 16, -1).transpose(0, 2, 1).reshape(8, -1).astype(np.int64)


def pick8(x, idx, run):
    r = np.arange(len(x))
    return x[r[:, None], idx[r % (8 * run) // run]]


E2M1 = np.array([0.0, 0.5, 1.0, 1.5, 2.0, 3.0, 4.0, 6.0, -0.0, -0.5, -1.0, -1.5, -2.0, -3.0, -4.0, -6.0])


def pack_weight(w, fmt):
    k, n = w.shape
    w = f64(np.asarray(w, np.float32).astype(ml_dtypes.bfloat16)).reshape(k // 32, 32, n)
    amax = np.abs(w).max(1)
    if fmt == "e4m3":
        byte = np.frexp(amax)[1] - 1 + 127 - 7
    else:
        mant, ex = np.frexp(amax / 6.0)
        byte = np.where(mant > 0.5, ex, ex - 1) + 127
    byte = np.clip(np.where(amax > 0, byte, 1), 1, 254)
    scaled = (w * np.exp2(127.0 - byte)[:, None, :]).reshape(k, n).astype(np.float32)
    by_word = np.ascontiguousarray(scaled.reshape(k // 512, 128, 4, n).transpose(0, 1, 3, 2))
    if fmt == "e4m3":
        words = by_word.astype(ml_dtypes.float8_e4m3fn).view(np.uint8)
    else:
        c = by_word.astype(ml_dtypes.float4_e2m1fn).view(np.uint8) & 0xF
        words = (c[..., 0::2] | (c[..., 1::2] << 4)).reshape(k // 512, 128, 2 * n)
    return np.ascontiguousarray(words), np.ascontiguousarray(byte.astype(np.uint8).reshape(k // 512, 16, n))


def unpack_weight(words, scales, fmt):
    g, _, n = scales.shape
    words = np.ascontiguousarray(words).reshape(g, 128, n, -1)
    if fmt == "e4m3":
        vals = words.view(ml_dtypes.float8_e4m3fn).astype(np.float64)
    else:
        nib = np.empty((g, 128, n, 4), np.uint8)
        nib[..., 0::2] = words & 0xF
        nib[..., 1::2] = words >> 4
        vals = E2M1[nib]
    vals = vals * np.repeat(np.exp2(scales.astype(np.float64) - 127.0), 8, axis=1)[..., None]
    return vals.transpose(0, 1, 3, 2).reshape(g * 512, n)


D, T, U, X, S, I, Q = 512, 1024, 1024, 1024, 1024, 512, 128


def setup_inputs():
    n = np.random.standard_normal
    idx = np.stack([np.random.permutation(T)[:I] for _ in range(8)])
    idx2 = np.stack([np.random.permutation(U)[:I] for _ in range(8)])
    idx3 = np.stack([np.random.permutation(X)[:I] for _ in range(8)])
    idx4 = np.stack([np.random.permutation(U)[:I] for _ in range(8)])
    idx5 = np.stack([np.random.permutation(S)[:I] for _ in range(8)])
    fd = mx_kscale(D)
    keysp = pack_weight(n((D, T)) / fd[:, None], "e4m3")
    notesp = pack_weight(n((D, U)) / fd[:, None], "e2m1")
    usersp = pack_weight(n((D, X)) / fd[:, None], "e4m3")
    shelvesp = pack_weight(n((D, S)) / fd[:, None], "e2m1")
    return {
        "query": (n((D, Q)) * 1.0 / np.sqrt(D) * fd[:, None]).astype(np.float32),
        "keys_words": keysp[0],
        "keys_scales": keysp[1],
        "notes_words": notesp[0],
        "notes_scales": notesp[1],
        "users_words": usersp[0],
        "users_scales": usersp[1],
        "shelves_words": shelvesp[0],
        "shelves_scales": shelvesp[1],
        "offs": striped8(idx),
        "offs2": striped8(idx2),
        "offs3": striped8(idx3),
        "offs4": striped8(idx4),
        "offs5": striped8(idx5),
    }


def reference(query, keys_words, keys_scales, notes_words, notes_scales, users_words, users_scales, shelves_words, shelves_scales, offs, offs2, offs3, offs4, offs5):
    idx = unstriped8(offs)
    idx2 = unstriped8(offs2)
    idx3 = unstriped8(offs3)
    idx4 = unstriped8(offs4)
    idx5 = unstriped8(offs5)
    keysu = unpack_weight(keys_words, keys_scales, "e4m3")
    notesu = unpack_weight(notes_words, notes_scales, "e2m1")
    usersu = unpack_weight(users_words, users_scales, "e4m3")
    shelvesu = unpack_weight(shelves_words, shelves_scales, "e2m1")
    queryq = mxq(f64(query), 0, "e4m3")
    a = queryq.T @ keysu
    b = queryq.T @ notesu
    c0 = queryq.T @ usersu
    d0 = queryq.T @ shelvesu
    ta = np.max(a, axis=1, keepdims=True)
    e1 = np.exp(pick8(a, idx, 16) - ta)
    w = pick8(c0, idx3, 16) - e1 * 2.0
    f1 = np.zeros((Q, U))
    f1[np.arange(Q)[:, None], idx2[np.arange(Q) % 128 // 16]] = w
    bb = b + f1
    y = np.minimum(pick8(bb, idx4, 16), pick8(d0, idx5, 16))
    return y

@@ -1,0 +1,137 @@
+from contextlib import ExitStack
+
+import concourse.mybir as mybir
+
+F32 = mybir.dt.float32
+BF16 = mybir.dt.bfloat16
+I32 = mybir.dt.int32
+U32 = mybir.dt.uint32
+U16 = mybir.dt.uint16
+U8 = mybir.dt.uint8
+FP8X4 = mybir.dt.float8_e4m3fn_x4
+FP4X4 = mybir.dt.float4_e2m1fn_x4
+ALU = mybir.AluOpType
+ACT = mybir.ActivationFunctionType
+AX = mybir.AxisListType
+
+P = 128
+D, POOL, SLOTS, ROWS = 512, 1024, 512, 128
+HALF = SLOTS // 2
+HCOL = HALF // 16
+FLOPS = 2 * D * ROWS * 4 * POOL
+
+
+def tile_attend_escorted_four_kernel(tc, query, keys_words, keys_scales, notes_words, notes_scales,
+                                      users_words, users_scales, shelves_words, shelves_scales,
+                                      offs, offs2, offs3, offs4, offs5, out):
+    nc = tc.nc
+    with ExitStack() as ctx:
+        sb = ctx.enter_context(tc.tile_pool(name="sb", bufs=1))
+        ps = ctx.enter_context(tc.psum_pool(name="ps", bufs=1))
+
+        def load_scales(queue, scales, name):
+            plane = sb.tile([P, POOL], U8, name=name, align_bytes=64)
+            for quad in range(4):
+                queue.dma_start(out=plane[32 * quad : 32 * quad + 4, :].bitcast(I32),
+                                in_=scales[0, 4 * quad : 4 * quad + 4, :].bitcast(I32))
+            return plane
+
+        def load_list(src, name):
+            t = sb.tile([P, SLOTS // 16], U16, name=name)
+            nc.sync.dma_start(t[:], src)
+            return t
+
+        def load_fp8(words, name):
+            t = sb.tile([P, POOL], U32, name=name, align_bytes=64)
+            nc.sync.dma_start(out=t[:].bitcast(I32), in_=words[0].rearrange("p n t -> p (n t)").bitcast(I32))
+            return t
+
+        def load_fp4(words, name):
+            t = sb.tile([P, 2 * POOL], U8, name=name, align_bytes=64)
+            nc.sync.dma_start(out=t[:].bitcast(I32), in_=words[0].bitcast(I32))
+            return t
+
+        q_raw = sb.tile([P, 4, ROWS], F32, name="q_raw")
+        nc.sync.dma_start(out=q_raw[:], in_=query.rearrange("(p j) w -> p j w", j=4))
+        keys_plane = load_scales(nc.sync, keys_scales, "keys_plane")
+        keys_codes = load_fp8(keys_words, "keys_codes")
+        users_codes = load_fp8(users_words, "users_codes")
+        users_plane = load_scales(nc.sync, users_scales, "users_plane")
+        token_list = load_list(offs, "token_list")
+        user_list = load_list(offs3, "user_list")
+        put_list = load_list(offs2, "put_list")
+        shelves_codes = load_fp4(shelves_words, "shelves_codes")
+        shelves_plane = load_scales(nc.sync, shelves_scales, "shelves_plane")
+        shelf_list = load_list(offs5, "shelf_list")
+        notes_codes = load_fp4(notes_words, "notes_codes")
+        notes_plane = load_scales(nc.sync, notes_scales, "notes_plane")
+        note_list = load_list(offs4, "note_list")
+
+        f1 = sb.tile([P, POOL], F32, name="f1")
+        nc.vector.memset(f1[:], 0.0)
+
+        q_bf = sb.tile([P, ROWS, 4], BF16, name="q_bf", align_bytes=64)
+        nc.scalar.activation(q_bf[:, 0:48, :], q_raw[:, :, 0:48].rearrange("p j w -> p w j"), ACT.Copy)
+        nc.vector.tensor_copy(out=q_bf[:, 48:, :], in_=q_raw[:, :, 48:].rearrange("p j w -> p w j"))
+        q_codes = sb.tile([P, ROWS], U32, name="q_codes", align_bytes=64)
+        q_plane = sb.tile([P, ROWS], U8, name="q_plane", align_bytes=64)
+        nc.vector.quantize_mx(out=q_codes[:].bitcast(FP8X4), scales=q_plane[:],
+                              in_=q_bf[:].rearrange("p w j -> p (w j)"))
+
+        def score(bank, codes, plane, lo, hi, fp4):
+            acc = ps.tile([P, hi - lo], F32, name="bank%d" % bank, tag="bank%d" % bank)
+            rhs = codes[:, 2 * lo : 2 * hi].bitcast(FP4X4) if fp4 else codes[:, lo:hi].bitcast(FP8X4)
+            nc.tensor.matmul_mx(out=acc[:], lhsT=q_codes[:].bitcast(FP8X4), lhsT_scale=q_plane[:],
+                                rhs=rhs, rhs_scale=plane[:, lo:hi], start=True, stop=True)
+            return acc
+
+        a_sb = sb.tile([P, POOL], F32, name="a_sb")
+        part_max = sb.tile([P, 4], F32, name="part_max")
+        for c in range(4):
+            acc = score(c, keys_codes, keys_plane, 256 * c, 256 * (c + 1), False)
+            nc.vector.tensor_reduce(out=part_max[:, c : c + 1], in_=acc[:], axis=AX.X, op=ALU.max)
+            nc.scalar.activation(a_sb[:, 256 * c : 256 * (c + 1)], acc[:], ACT.Copy)
+        c_sb = sb.tile([P, POOL], F32, name="c_sb")
+        neg_ta = sb.tile([P, 1], F32, name="neg_ta")
+        for c in range(4):
+            acc = score(4 + c, users_codes, users_plane, 256 * c, 256 * (c + 1), False)
+            nc.vector.tensor_copy(out=c_sb[:, 256 * c : 256 * (c + 1)], in_=acc[:])
+            if c == 0:
+                nc.vector.tensor_reduce(out=neg_ta[:], in_=part_max[:], axis=AX.X, op=ALU.max, negate=True)
+
+        e1 = [sb.tile([P, HALF], F32, name="e1_%d" % h) for h in range(2)]
+        m2 = [sb.tile([P, HALF], F32, name="m2_%d" % h) for h in range(2)]
+        cg = [sb.tile([P, HALF], F32, name="cg_%d" % h) for h in range(2)]
+
+        def half(lst, h):
+            return lst[:, h * HCOL : (h + 1) * HCOL]
+
+        nc.scalar.activation(e1[0][:], a_sb[:].indirect(half(token_list, 0)), ACT.Exp, bias=neg_ta[:])
+        nc.scalar.activation(m2[0][:], e1[0][:], ACT.Copy, scale=-2.0)
+        nc.vector.tensor_copy(out=cg[0][:], in_=c_sb[:].indirect(half(user_list, 0)))
+        nc.vector.tensor_tensor(f1[:].indirect(half(put_list, 0)), cg[0][:], m2[0][:], ALU.add)
+
+        nc.scalar.activation(e1[1][:], a_sb[:].indirect(half(token_list, 1)), ACT.Exp, bias=neg_ta[:])
+        nc.scalar.activation(cg[1][:], c_sb[:].indirect(half(user_list, 1)), ACT.Copy)
+        nc.scalar.activation(m2[1][:], e1[1][:], ACT.Copy, scale=-2.0)
+        nc.vector.tensor_tensor(f1[:].indirect(half(put_list, 1)), cg[1][:], m2[1][:], ALU.add)
+
+        d_sb = sb.tile([P, POOL], F32, name="d_sb")
+        for n in range(2):
+            acc = score(n, shelves_codes, shelves_plane, 512 * n, 512 * (n + 1), True)
+            nc.scalar.activation(d_sb[:, 512 * n : 512 * (n + 1)], acc[:], ACT.Copy)
+        dg = sb.tile([P, SLOTS], F32, name="dg")
+        nc.scalar.activation(dg[:], d_sb[:].indirect(shelf_list[:]), ACT.Copy)
+
+        bb = sb.tile([P, POOL], F32, name="bb")
+        for n in range(2):
+            acc = score(2 + n, notes_codes, notes_plane, 512 * n, 512 * (n + 1), True)
+            nc.vector.tensor_tensor(bb[:, 512 * n : 512 * (n + 1)], acc[:], f1[:, 512 * n : 512 * (n + 1)], ALU.add)
+
+        bg = [sb.tile([P, HALF], F32, name="bg_%d" % h) for h in range(2)]
+        y = [sb.tile([P, HALF], F32, name="y_%d" % h) for h in range(2)]
+        nc.vector.tensor_copy(out=bg[0][:], in_=bb[:].indirect(half(note_list, 0)))
+        nc.scalar.activation(bg[1][:], bb[:].indirect(half(note_list, 1)), ACT.Copy)
+        for h, queue in ((1, nc.sync), (0, nc.scalar)):
+            nc.vector.tensor_tensor(y[h][:], bg[h][:], dg[:, h * HALF : (h + 1) * HALF], ALU.min)
+            queue.dma_start(out=out[:, h * HALF : (h + 1) * HALF], in_=y[h][:])

@@ -36,14 +36,21 @@ def tile_attend_escorted_four_kernel(tc, query, keys_words, keys_scales, notes_w
                                 in_=scales[0, 4 * quad : 4 * quad + 4, :].bitcast(I32))
             return plane
 
+        def load_packed_scales(queue, plane, scales, quads):
+            for quad in quads:
+                rows = scales[0, 4 * quad : 4 * quad + 4, :].bitcast(I32)
+                queue.dma_start(out=plane[32 * quad : 32 * quad + 16, :].bitcast(I32),
+                                in_=rows.rearrange("r (j n) -> j r n", j=4))
+
         def load_list(src, name):
             t = sb.tile([P, SLOTS // 16], U16, name=name)
             nc.sync.dma_start(t[:], src)
             return t
 
-        def load_fp8(words, name):
-            t = sb.tile([P, POOL], U32, name=name, align_bytes=64)
-            nc.sync.dma_start(out=t[:].bitcast(I32), in_=words[0].rearrange("p n t -> p (n t)").bitcast(I32))
+        def load_fp8(words, name, part):
+            t = sb.tile([P, POOL // 2], U32, name=name, align_bytes=64)
+            src = words[0].rearrange("p n t -> p (n t)").bitcast(I32)
+            nc.sync.dma_start(out=t[:].bitcast(I32), in_=src[:, part * (POOL // 2) : (part + 1) * (POOL // 2)])
             return t
 
         def load_fp4(words, name):
@@ -53,10 +60,14 @@ def tile_attend_escorted_four_kernel(tc, query, keys_words, keys_scales, notes_w
 
         q_raw = sb.tile([P, 4, ROWS], F32, name="q_raw")
         nc.sync.dma_start(out=q_raw[:], in_=query.rearrange("(p j) w -> p j w", j=4))
-        keys_plane = load_scales(nc.sync, keys_scales, "keys_plane")
-        keys_codes = load_fp8(keys_words, "keys_codes")
-        users_codes = load_fp8(users_words, "users_codes")
-        users_plane = load_scales(nc.sync, users_scales, "users_plane")
+        keys_plane = sb.tile([P, POOL // 4], U8, name="keys_plane", align_bytes=64)
+        users_plane = sb.tile([P, POOL // 4], U8, name="users_plane", align_bytes=64)
+        load_packed_scales(nc.sync, keys_plane, keys_scales, range(4))
+        keys_codes = [load_fp8(keys_words, "keys_codes%d" % n, n) for n in range(2)]
+        users_codes = [load_fp8(users_words, "users_codes0", 0)]
+        load_packed_scales(nc.gpsimd, users_plane, users_scales, (0,))
+        load_packed_scales(nc.sync, users_plane, users_scales, (1, 2, 3))
+        users_codes.append(load_fp8(users_words, "users_codes1", 1))
         token_list = load_list(offs, "token_list")
         user_list = load_list(offs3, "user_list")
         put_list = load_list(offs2, "put_list")
@@ -67,22 +78,22 @@ def tile_attend_escorted_four_kernel(tc, query, keys_words, keys_scales, notes_w
         notes_plane = load_scales(nc.sync, notes_scales, "notes_plane")
         note_list = load_list(offs4, "note_list")
 
-        f1 = sb.tile([P, POOL], F32, name="f1")
-        nc.vector.memset(f1[:], 0.0)
-
-        q_bf = sb.tile([P, ROWS, 4], BF16, name="q_bf", align_bytes=64)
-        nc.scalar.activation(q_bf[:, 0:48, :], q_raw[:, :, 0:48].rearrange("p j w -> p w j"), ACT.Copy)
-        nc.vector.tensor_copy(out=q_bf[:, 48:, :], in_=q_raw[:, :, 48:].rearrange("p j w -> p w j"))
+        q_bf = sb.tile([P, ROWS, 4], BF16, name="q_bf", tag="q_bf", align_bytes=64)
+        nc.scalar.activation(q_bf[:, 0:64, :], q_raw[:, :, 0:64].rearrange("p j w -> p w j"), ACT.Copy)
+        nc.vector.tensor_copy(out=q_bf[:, 64:, :], in_=q_raw[:, :, 64:].rearrange("p j w -> p w j"))
         q_codes = sb.tile([P, ROWS], U32, name="q_codes", align_bytes=64)
         q_plane = sb.tile([P, ROWS], U8, name="q_plane", align_bytes=64)
         nc.vector.quantize_mx(out=q_codes[:].bitcast(FP8X4), scales=q_plane[:],
                               in_=q_bf[:].rearrange("p w j -> p (w j)"))
 
+        f1 = sb.tile([P, POOL], F32, name="f1", tag="q_bf", align_bytes=64)
+        nc.gpsimd.memset(f1[:], 0.0)
+
         def score(bank, codes, plane, lo, hi, fp4):
             acc = ps.tile([P, hi - lo], F32, name="bank%d" % bank, tag="bank%d" % bank)
-            rhs = codes[:, 2 * lo : 2 * hi].bitcast(FP4X4) if fp4 else codes[:, lo:hi].bitcast(FP8X4)
+            rhs = codes[:, 2 * lo : 2 * hi].bitcast(FP4X4) if fp4 else codes[lo // 512][:, lo % 512 : lo % 512 + hi - lo].bitcast(FP8X4)
             nc.tensor.matmul_mx(out=acc[:], lhsT=q_codes[:].bitcast(FP8X4), lhsT_scale=q_plane[:],
-                                rhs=rhs, rhs_scale=plane[:, lo:hi], start=True, stop=True)
+                                rhs=rhs, rhs_scale=plane[:, lo:hi] if fp4 else plane[lo // 64 : P, :], start=True, stop=True)
             return acc
 
         a_sb = sb.tile([P, POOL], F32, name="a_sb")
@@ -91,7 +102,7 @@ def tile_attend_escorted_four_kernel(tc, query, keys_words, keys_scales, notes_w
             acc = score(c, keys_codes, keys_plane, 256 * c, 256 * (c + 1), False)
             nc.vector.tensor_reduce(out=part_max[:, c : c + 1], in_=acc[:], axis=AX.X, op=ALU.max)
             nc.scalar.activation(a_sb[:, 256 * c : 256 * (c + 1)], acc[:], ACT.Copy)
-        c_sb = sb.tile([P, POOL], F32, name="c_sb")
+        c_sb = sb.tile([P, POOL], F32, name="c_sb", tag="c_sb")
         neg_ta = sb.tile([P, 1], F32, name="neg_ta")
         for c in range(4):
             acc = score(4 + c, users_codes, users_plane, 256 * c, 256 * (c + 1), False)
@@ -99,7 +110,7 @@ def tile_attend_escorted_four_kernel(tc, query, keys_words, keys_scales, notes_w
             if c == 0:
                 nc.vector.tensor_reduce(out=neg_ta[:], in_=part_max[:], axis=AX.X, op=ALU.max, negate=True)
 
-        e1 = [sb.tile([P, HALF], F32, name="e1_%d" % h) for h in range(2)]
+        e1 = [sb.tile([P, HALF], F32, name="e1_0")]
         m2 = [sb.tile([P, HALF], F32, name="m2_%d" % h) for h in range(2)]
         cg = [sb.tile([P, HALF], F32, name="cg_%d" % h) for h in range(2)]
 
@@ -107,25 +118,26 @@ def tile_attend_escorted_four_kernel(tc, query, keys_words, keys_scales, notes_w
             return lst[:, h * HCOL : (h + 1) * HCOL]
 
         nc.scalar.activation(e1[0][:], a_sb[:].indirect(half(token_list, 0)), ACT.Exp, bias=neg_ta[:])
-        nc.scalar.activation(m2[0][:], e1[0][:], ACT.Copy, scale=-2.0)
-        nc.vector.tensor_copy(out=cg[0][:], in_=c_sb[:].indirect(half(user_list, 0)))
+        nc.scalar.activation(cg[0][:], c_sb[:].indirect(half(user_list, 0)), ACT.Copy)
+        nc.vector.tensor_scalar(m2[0][:], e1[0][:], -2.0, None, ALU.mult)
         nc.vector.tensor_tensor(f1[:].indirect(half(put_list, 0)), cg[0][:], m2[0][:], ALU.add)
 
-        nc.scalar.activation(e1[1][:], a_sb[:].indirect(half(token_list, 1)), ACT.Exp, bias=neg_ta[:])
         nc.scalar.activation(cg[1][:], c_sb[:].indirect(half(user_list, 1)), ACT.Copy)
+        e1.append(sb.tile([P, HALF], F32, name="e1_1", tag="c_sb"))
+        nc.scalar.activation(e1[1][:], a_sb[:].indirect(half(token_list, 1)), ACT.Exp, bias=neg_ta[:])
         nc.scalar.activation(m2[1][:], e1[1][:], ACT.Copy, scale=-2.0)
         nc.vector.tensor_tensor(f1[:].indirect(half(put_list, 1)), cg[1][:], m2[1][:], ALU.add)
 
         d_sb = sb.tile([P, POOL], F32, name="d_sb")
         for n in range(2):
-            acc = score(n, shelves_codes, shelves_plane, 512 * n, 512 * (n + 1), True)
+            acc = score(4 + n, shelves_codes, shelves_plane, 512 * n, 512 * (n + 1), True)
             nc.scalar.activation(d_sb[:, 512 * n : 512 * (n + 1)], acc[:], ACT.Copy)
         dg = sb.tile([P, SLOTS], F32, name="dg")
         nc.scalar.activation(dg[:], d_sb[:].indirect(shelf_list[:]), ACT.Copy)
 
         bb = sb.tile([P, POOL], F32, name="bb")
         for n in range(2):
-            acc = score(2 + n, notes_codes, notes_plane, 512 * n, 512 * (n + 1), True)
+            acc = score(6 + n, notes_codes, notes_plane, 512 * n, 512 * (n + 1), True)
             nc.vector.tensor_tensor(bb[:, 512 * n : 512 * (n + 1)], acc[:], f1[:, 512 * n : 512 * (n + 1)], ALU.add)
 
         bg = [sb.tile([P, HALF], F32, name="bg_%d" % h) for h in range(2)]

@@ -47,11 +47,11 @@ def tile_attend_escorted_four_kernel(tc, query, keys_words, keys_scales, notes_w
             nc.sync.dma_start(t[:], src)
             return t
 
-        def load_fp8(words, name, part):
-            t = sb.tile([P, POOL // 2], U32, name=name, align_bytes=64)
+        def load_fp8(words, name, lo, hi):
+            t = sb.tile([P, hi - lo], U32, name=name, align_bytes=64)
             src = words[0].rearrange("p n t -> p (n t)").bitcast(I32)
-            nc.sync.dma_start(out=t[:].bitcast(I32), in_=src[:, part * (POOL // 2) : (part + 1) * (POOL // 2)])
-            return t
+            nc.sync.dma_start(out=t[:].bitcast(I32), in_=src[:, lo:hi])
+            return [t[:, n : n + 256] for n in range(0, hi - lo, 256)]
 
         def load_fp4(words, name):
             t = sb.tile([P, 2 * POOL], U8, name=name, align_bytes=64)
@@ -63,11 +63,11 @@ def tile_attend_escorted_four_kernel(tc, query, keys_words, keys_scales, notes_w
         keys_plane = sb.tile([P, POOL // 4], U8, name="keys_plane", align_bytes=64)
         users_plane = sb.tile([P, POOL // 4], U8, name="users_plane", align_bytes=64)
         load_packed_scales(nc.sync, keys_plane, keys_scales, range(4))
-        keys_codes = [load_fp8(keys_words, "keys_codes%d" % n, n) for n in range(2)]
-        users_codes = [load_fp8(users_words, "users_codes0", 0)]
+        keys_codes = load_fp8(keys_words, "keys_codes0", 0, 512) + load_fp8(keys_words, "keys_codes1", 512, 1024)
+        users_codes = load_fp8(users_words, "users_codes0", 0, 768)
         load_packed_scales(nc.gpsimd, users_plane, users_scales, (0,))
         load_packed_scales(nc.sync, users_plane, users_scales, (1, 2, 3))
-        users_codes.append(load_fp8(users_words, "users_codes1", 1))
+        users_codes.extend(load_fp8(users_words, "users_codes1", 768, 1024))
         token_list = load_list(offs, "token_list")
         user_list = load_list(offs3, "user_list")
         put_list = load_list(offs2, "put_list")
@@ -91,7 +91,7 @@ def tile_attend_escorted_four_kernel(tc, query, keys_words, keys_scales, notes_w
 
         def score(bank, codes, plane, lo, hi, fp4):
             acc = ps.tile([P, hi - lo], F32, name="bank%d" % bank, tag="bank%d" % bank)
-            rhs = codes[:, 2 * lo : 2 * hi].bitcast(FP4X4) if fp4 else codes[lo // 512][:, lo % 512 : lo % 512 + hi - lo].bitcast(FP8X4)
+            rhs = codes[:, 2 * lo : 2 * hi].bitcast(FP4X4) if fp4 else codes[lo // 256].bitcast(FP8X4)
             nc.tensor.matmul_mx(out=acc[:], lhsT=q_codes[:].bitcast(FP8X4), lhsT_scale=q_plane[:],
                                 rhs=rhs, rhs_scale=plane[:, lo:hi] if fp4 else plane[lo // 64 : P, :], start=True, stop=True)
             return acc
@@ -102,7 +102,7 @@ def tile_attend_escorted_four_kernel(tc, query, keys_words, keys_scales, notes_w
             acc = score(c, keys_codes, keys_plane, 256 * c, 256 * (c + 1), False)
             nc.vector.tensor_reduce(out=part_max[:, c : c + 1], in_=acc[:], axis=AX.X, op=ALU.max)
             nc.scalar.activation(a_sb[:, 256 * c : 256 * (c + 1)], acc[:], ACT.Copy)
-        c_sb = sb.tile([P, POOL], F32, name="c_sb", tag="c_sb")
+        c_sb = sb.tile([P, POOL], F32, name="c_sb")
         neg_ta = sb.tile([P, 1], F32, name="neg_ta")
         for c in range(4):
             acc = score(4 + c, users_codes, users_plane, 256 * c, 256 * (c + 1), False)
@@ -110,23 +110,20 @@ def tile_attend_escorted_four_kernel(tc, query, keys_words, keys_scales, notes_w
             if c == 0:
                 nc.vector.tensor_reduce(out=neg_ta[:], in_=part_max[:], axis=AX.X, op=ALU.max, negate=True)
 
-        e1 = [sb.tile([P, HALF], F32, name="e1_0")]
-        m2 = [sb.tile([P, HALF], F32, name="m2_%d" % h) for h in range(2)]
-        cg = [sb.tile([P, HALF], F32, name="cg_%d" % h) for h in range(2)]
+        e1 = [sb.tile([P, HALF], F32, name="e1_%d" % h) for h in range(2)]
+        m2 = sb.tile([P, SLOTS], F32, name="m2")
+        cg = sb.tile([P, SLOTS], F32, name="cg")
 
         def half(lst, h):
             return lst[:, h * HCOL : (h + 1) * HCOL]
 
-        nc.scalar.activation(e1[0][:], a_sb[:].indirect(half(token_list, 0)), ACT.Exp, bias=neg_ta[:])
-        nc.scalar.activation(cg[0][:], c_sb[:].indirect(half(user_list, 0)), ACT.Copy)
-        nc.vector.tensor_scalar(m2[0][:], e1[0][:], -2.0, None, ALU.mult)
-        nc.vector.tensor_tensor(f1[:].indirect(half(put_list, 0)), cg[0][:], m2[0][:], ALU.add)
-
-        nc.scalar.activation(cg[1][:], c_sb[:].indirect(half(user_list, 1)), ACT.Copy)
-        e1.append(sb.tile([P, HALF], F32, name="e1_1", tag="c_sb"))
-        nc.scalar.activation(e1[1][:], a_sb[:].indirect(half(token_list, 1)), ACT.Exp, bias=neg_ta[:])
-        nc.scalar.activation(m2[1][:], e1[1][:], ACT.Copy, scale=-2.0)
-        nc.vector.tensor_tensor(f1[:].indirect(half(put_list, 1)), cg[1][:], m2[1][:], ALU.add)
+        for h in range(2):
+            nc.scalar.activation(e1[h][:], a_sb[:].indirect(half(token_list, h)), ACT.Exp, bias=neg_ta[:])
+        nc.vector.tensor_scalar(m2[:, 0:HALF], e1[0][:], -2.0, None, ALU.mult)
+        nc.gpsimd.tensor_scalar(m2[:, HALF:], e1[1][:], -2.0, 0.0, ALU.mult, ALU.add)
+        nc.vector.tensor_copy(out=cg[:, 0:HALF], in_=c_sb[:].indirect(half(user_list, 0)))
+        nc.scalar.activation(cg[:, HALF:], c_sb[:].indirect(half(user_list, 1)), ACT.Copy)
+        nc.vector.tensor_tensor(f1[:].indirect(put_list[:]), cg[:], m2[:], ALU.add)
 
         d_sb = sb.tile([P, POOL], F32, name="d_sb")
         for n in range(2):

from contextlib import ExitStack

import concourse.mybir as mybir

F32 = mybir.dt.float32
BF16 = mybir.dt.bfloat16
I32 = mybir.dt.int32
U32 = mybir.dt.uint32
U16 = mybir.dt.uint16
U8 = mybir.dt.uint8
FP8X4 = mybir.dt.float8_e4m3fn_x4
FP4X4 = mybir.dt.float4_e2m1fn_x4
ALU = mybir.AluOpType
ACT = mybir.ActivationFunctionType
AX = mybir.AxisListType

P = 128
D, POOL, SLOTS, ROWS = 512, 1024, 512, 128
HALF = SLOTS // 2
HCOL = HALF // 16
FLOPS = 2 * D * ROWS * 4 * POOL


def tile_attend_escorted_four_kernel(tc, query, keys_words, keys_scales, notes_words, notes_scales,
                                      users_words, users_scales, shelves_words, shelves_scales,
                                      offs, offs2, offs3, offs4, offs5, out):
    nc = tc.nc
    with ExitStack() as ctx:
        sb = ctx.enter_context(tc.tile_pool(name="sb", bufs=1))
        ps = ctx.enter_context(tc.psum_pool(name="ps", bufs=1))

        def load_scales(queue, scales, name):
            plane = sb.tile([P, POOL], U8, name=name, align_bytes=64)
            for quad in range(4):
                queue.dma_start(out=plane[32 * quad : 32 * quad + 4, :].bitcast(I32),
                                in_=scales[0, 4 * quad : 4 * quad + 4, :].bitcast(I32))
            return plane

        def load_packed_scales(queue, plane, scales, quads):
            for quad in quads:
                rows = scales[0, 4 * quad : 4 * quad + 4, :].bitcast(I32)
                queue.dma_start(out=plane[32 * quad : 32 * quad + 16, :].bitcast(I32),
                                in_=rows.rearrange("r (j n) -> j r n", j=4))

        def load_list(src, name):
            t = sb.tile([P, SLOTS // 16], U16, name=name)
            nc.sync.dma_start(t[:], src)
            return t

        def load_fp8(words, name, lo, hi):
            t = sb.tile([P, hi - lo], U32, name=name, align_bytes=64)
            src = words[0].rearrange("p n t -> p (n t)").bitcast(I32)
            nc.sync.dma_start(out=t[:].bitcast(I32), in_=src[:, lo:hi])
            return [t[:, n : n + 256] for n in range(0, hi - lo, 256)]

        def load_fp4(words, name):
            t = sb.tile([P, 2 * POOL], U8, name=name, align_bytes=64)
            nc.sync.dma_start(out=t[:].bitcast(I32), in_=words[0].bitcast(I32))
            return t

        q_raw = sb.tile([P, 4, ROWS], F32, name="q_raw")
        nc.sync.dma_start(out=q_raw[:], in_=query.rearrange("(p j) w -> p j w", j=4))
        keys_plane = sb.tile([P, POOL // 4], U8, name="keys_plane", align_bytes=64)
        users_plane = sb.tile([P, POOL // 4], U8, name="users_plane", align_bytes=64)
        load_packed_scales(nc.sync, keys_plane, keys_scales, range(4))
        keys_codes = load_fp8(keys_words, "keys_codes0", 0, 512) + load_fp8(keys_words, "keys_codes1", 512, 1024)
        users_codes = load_fp8(users_words, "users_codes0", 0, 768)
        load_packed_scales(nc.gpsimd, users_plane, users_scales, (0,))
        load_packed_scales(nc.sync, users_plane, users_scales, (1, 2, 3))
        users_codes.extend(load_fp8(users_words, "users_codes1", 768, 1024))
        token_list = load_list(offs, "token_list")
        user_list = load_list(offs3, "user_list")
        put_list = load_list(offs2, "put_list")
        shelves_codes = load_fp4(shelves_words, "shelves_codes")
        shelves_plane = load_scales(nc.sync, shelves_scales, "shelves_plane")
        shelf_list = load_list(offs5, "shelf_list")
        notes_codes = load_fp4(notes_words, "notes_codes")
        notes_plane = load_scales(nc.sync, notes_scales, "notes_plane")
        note_list = load_list(offs4, "note_list")

        q_bf = sb.tile([P, ROWS, 4], BF16, name="q_bf", tag="q_bf", align_bytes=64)
        nc.scalar.activation(q_bf[:, 0:64, :], q_raw[:, :, 0:64].rearrange("p j w -> p w j"), ACT.Copy)
        nc.vector.tensor_copy(out=q_bf[:, 64:, :], in_=q_raw[:, :, 64:].rearrange("p j w -> p w j"))
        q_codes = sb.tile([P, ROWS], U32, name="q_codes", align_bytes=64)
        q_plane = sb.tile([P, ROWS], U8, name="q_plane", align_bytes=64)
        nc.vector.quantize_mx(out=q_codes[:].bitcast(FP8X4), scales=q_plane[:],
                              in_=q_bf[:].rearrange("p w j -> p (w j)"))

        f1 = sb.tile([P, POOL], F32, name="f1", tag="q_bf", align_bytes=64)
        nc.gpsimd.memset(f1[:], 0.0)

        def score(bank, codes, plane, lo, hi, fp4):
            acc = ps.tile([P, hi - lo], F32, name="bank%d" % bank, tag="bank%d" % bank)
            rhs = codes[:, 2 * lo : 2 * hi].bitcast(FP4X4) if fp4 else codes[lo // 256].bitcast(FP8X4)
            nc.tensor.matmul_mx(out=acc[:], lhsT=q_codes[:].bitcast(FP8X4), lhsT_scale=q_plane[:],
                                rhs=rhs, rhs_scale=plane[:, lo:hi] if fp4 else plane[lo // 64 : P, :], start=True, stop=True)
            return acc

        a_sb = sb.tile([P, POOL], F32, name="a_sb")
        part_max = sb.tile([P, 4], F32, name="part_max")
        for c in range(4):
            acc = score(c, keys_codes, keys_plane, 256 * c, 256 * (c + 1), False)
            nc.vector.tensor_reduce(out=part_max[:, c : c + 1], in_=acc[:], axis=AX.X, op=ALU.max)
            nc.scalar.activation(a_sb[:, 256 * c : 256 * (c + 1)], acc[:], ACT.Copy)
        c_sb = sb.tile([P, POOL], F32, name="c_sb")
        neg_ta = sb.tile([P, 1], F32, name="neg_ta")
        for c in range(4):
            acc = score(4 + c, users_codes, users_plane, 256 * c, 256 * (c + 1), False)
            nc.vector.tensor_copy(out=c_sb[:, 256 * c : 256 * (c + 1)], in_=acc[:])
            if c == 0:
                nc.vector.tensor_reduce(out=neg_ta[:], in_=part_max[:], axis=AX.X, op=ALU.max, negate=True)

        e1 = [sb.tile([P, HALF], F32, name="e1_%d" % h) for h in range(2)]
        m2 = sb.tile([P, SLOTS], F32, name="m2")
        cg = sb.tile([P, SLOTS], F32, name="cg")

        def half(lst, h):
            return lst[:, h * HCOL : (h + 1) * HCOL]

        for h in range(2):
            nc.scalar.activation(e1[h][:], a_sb[:].indirect(half(token_list, h)), ACT.Exp, bias=neg_ta[:])
        nc.vector.tensor_scalar(m2[:, 0:HALF], e1[0][:], -2.0, None, ALU.mult)
        nc.gpsimd.tensor_scalar(m2[:, HALF:], e1[1][:], -2.0, 0.0, ALU.mult, ALU.add)
        nc.vector.tensor_copy(out=cg[:, 0:HALF], in_=c_sb[:].indirect(half(user_list, 0)))
        nc.scalar.activation(cg[:, HALF:], c_sb[:].indirect(half(user_list, 1)), ACT.Copy)
        nc.vector.tensor_tensor(f1[:].indirect(put_list[:]), cg[:], m2[:], ALU.add)

        d_sb = sb.tile([P, POOL], F32, name="d_sb")
        for n in range(2):
            acc = score(4 + n, shelves_codes, shelves_plane, 512 * n, 512 * (n + 1), True)
            nc.scalar.activation(d_sb[:, 512 * n : 512 * (n + 1)], acc[:], ACT.Copy)
        dg = sb.tile([P, SLOTS], F32, name="dg")
        nc.scalar.activation(dg[:], d_sb[:].indirect(shelf_list[:]), ACT.Copy)

        bb = sb.tile([P, POOL], F32, name="bb")
        for n in range(2):
            acc = score(6 + n, notes_codes, notes_plane, 512 * n, 512 * (n + 1), True)
            nc.vector.tensor_tensor(bb[:, 512 * n : 512 * (n + 1)], acc[:], f1[:, 512 * n : 512 * (n + 1)], ALU.add)

        bg = [sb.tile([P, HALF], F32, name="bg_%d" % h) for h in range(2)]
        y = [sb.tile([P, HALF], F32, name="y_%d" % h) for h in range(2)]
        nc.vector.tensor_copy(out=bg[0][:], in_=bb[:].indirect(half(note_list, 0)))
        nc.scalar.activation(bg[1][:], bb[:].indirect(half(note_list, 1)), ACT.Copy)
        for h, queue in ((1, nc.sync), (0, nc.scalar)):
            nc.vector.tensor_tensor(y[h][:], bg[h][:], dg[:, h * HALF : (h + 1) * HALF], ALU.min)
            queue.dma_start(out=out[:, h * HALF : (h + 1) * HALF], in_=y[h][:])
